import numpy as np
import ml_dtypes


def mxq(x, axis, fmt="e4m3"):
    dtype, down = {"e4m3": (ml_dtypes.float8_e4m3fn, 7), "e5m2": (ml_dtypes.float8_e5m2, 14)}[fmt]
    v = np.moveaxis(np.asarray(x, np.float32).astype(ml_dtypes.bfloat16).astype(np.float64), axis, -1)
    blocks = v.reshape(v.shape[:-1] + (-1, 32))
    amax = np.abs(blocks).max(-1, keepdims=True)
    byte = np.maximum(np.where(amax > 0, np.frexp(amax)[1] - 1 + 127, 0) - down, 1)
    scale = np.exp2(byte - 127.0)
    codes = (blocks / scale).astype(np.float32).astype(dtype).astype(np.float64)
    return np.moveaxis((codes * scale).reshape(v.shape), -1, axis)


WIDE = False


def mx_kscale(k):
    if not WIDE:
        return np.ones(k)
    levels = np.array([30, -30])
    if k % 512:
        return np.exp2(np.random.permutation(np.resize(levels, k // 32))).repeat(32)
    a = np.empty((k // 512, 16))
    for p in range(k // 512):
        a[p, :8] = np.random.permutation(np.resize(levels, 8))
        for g in range(8):
            far = levels[np.abs(levels - a[p, g]) >= 10]
            a[p, g + 8] = far[np.random.randint(len(far))]
    return np.exp2(a.ravel()).repeat(32)


def f64(x):
    return np.asarray(x).astype(np.float64)


def striped(idx):
    return np.tile(np.asarray(idx).reshape(-1, 16).T, (8, 1)).astype(np.uint16)


def unstriped(offs):
    return offs[:16].T.reshape(-1).astype(np.int64)


E2M1 = np.array([0.0, 0.5, 1.0, 1.5, 2.0, 3.0, 4.0, 6.0, -0.0, -0.5, -1.0, -1.5, -2.0, -3.0, -4.0, -6.0])


def pack_weight(w, fmt):
    k, n = w.shape
    w = f64(np.asarray(w, np.float32).astype(ml_dtypes.bfloat16)).reshape(k // 32, 32, n)
    amax = np.abs(w).max(1)
    if fmt in ("e4m3", "e5m2"):
        byte = np.frexp(amax)[1] - 1 + 127 - (7 if fmt == "e4m3" else 14)
    else:
        mant, ex = np.frexp(amax / 6.0)
        byte = np.where(mant > 0.5, ex, ex - 1) + 127
    byte = np.clip(np.where(amax > 0, byte, 1), 1, 254)
    scaled = (w * np.exp2(127.0 - byte)[:, None, :]).reshape(k, n).astype(np.float32)
    by_word = np.ascontiguousarray(scaled.reshape(k // 512, 128, 4, n).transpose(0, 1, 3, 2))
    if fmt in ("e4m3", "e5m2"):
        words = by_word.astype(ml_dtypes.float8_e4m3fn if fmt == "e4m3" else ml_dtypes.float8_e5m2).view(np.uint8)
    else:
        c = by_word.astype(ml_dtypes.float4_e2m1fn).view(np.uint8) & 0xF
        words = (c[..., 0::2] | (c[..., 1::2] << 4)).reshape(k // 512, 128, 2 * n)
    return np.ascontiguousarray(words), np.ascontiguousarray(byte.astype(np.uint8).reshape(k // 512, 16, n))


def unpack_weight(words, scales, fmt):
    g, _, n = scales.shape
    words = np.ascontiguousarray(words).reshape(g, 128, n, -1)
    if fmt in ("e4m3", "e5m2"):
        vals = words.view(ml_dtypes.float8_e4m3fn if fmt == "e4m3" else ml_dtypes.float8_e5m2).astype(np.float64)
    else:
        nib = np.empty((g, 128, n, 4), np.uint8)
        nib[..., 0::2] = words & 0xF
        nib[..., 1::2] = words >> 4
        vals = E2M1[nib]
    vals = vals * np.repeat(np.exp2(scales.astype(np.float64) - 127.0), 8, axis=1)[..., None]
    return vals.transpose(0, 1, 3, 2).reshape(g * 512, n)


K, F, T, Z, J, R, N = 512, 512, 1024, 1024, 256, 512, 256


def setup_inputs():
    n = np.random.standard_normal
    idx = np.random.permutation(T)[:J]
    idx2 = np.random.permutation(Z)[:J]
    idx3 = np.random.permutation(J)[:J]
    fk = mx_kscale(K)
    fr = mx_kscale(R)
    ff = mx_kscale(F)
    xtp = pack_weight(n((K, T)) / fk[:, None], "e5m2")
    wp = pack_weight(n((K, R)) * 1 / np.sqrt(K) * fk[:, None] * fr, "e2m1")
    xop = pack_weight(n((F, Z)) / ff[:, None], "e4m3")
    w2p = pack_weight(n((F, R)) * 1 / np.sqrt(F) * ff[:, None] * fr, "e2m1")
    wbp = pack_weight(n((R, N)) * 1 / np.sqrt(R) / fr[:, None], "e2m1")
    wcp = pack_weight(n((R, N)) * 1 / np.sqrt(R) / fr[:, None], "e4m3")
    return {
        "xt_words": xtp[0],
        "xt_scales": xtp[1],
        "w_words": wp[0],
        "w_scales": wp[1],
        "xo_words": xop[0],
        "xo_scales": xop[1],
        "w2_words": w2p[0],
        "w2_scales": w2p[1],
        "wb_words": wbp[0],
        "wb_scales": wbp[1],
        "wc_words": wcp[0],
        "wc_scales": wcp[1],
        "so": (np.random.uniform(0.5, 1.6, (N, 1))).astype(np.float32),
        "offs": striped(idx),
        "offs2": striped(idx2),
        "offs3": striped(idx3),
    }


def reference(xt_words, xt_scales, w_words, w_scales, xo_words, xo_scales, w2_words, w2_scales, wb_words, wb_scales, wc_words, wc_scales, so, offs, offs2, offs3):
    idx = unstriped(offs)
    idx2 = unstriped(offs2)
    idx3 = unstriped(offs3)
    xtu = unpack_weight(xt_words, xt_scales, "e5m2")
    wu = unpack_weight(w_words, w_scales, "e2m1")
    xou = unpack_weight(xo_words, xo_scales, "e4m3")
    w2u = unpack_weight(w2_words, w2_scales, "e2m1")
    wbu = unpack_weight(wb_words, wb_scales, "e2m1")
    wcu = unpack_weight(wc_words, wc_scales, "e4m3")
    xtidxg = xtu[:, idx]
    a = wu.T @ xtidxg
    xoidx2g = xou[:, idx2]
    b = w2u.T @ xoidx2g
    hid = np.abs(a - b)
    hidq = mxq(hid, 0, "e4m3")
    p = wbu.T @ hidq
    q = wcu.T @ hidq
    m0 = np.maximum(p, q)
    y = m0 - m0[:, idx3] * f64(so)
    return y

@@ -1,0 +1,183 @@
+from contextlib import ExitStack
+
+import concourse.mybir as mybir
+
+K, T, J, R, N = 512, 1024, 256, 512, 256
+FLOPS = 2 * K * R * J * 2 + 2 * R * N * J * 2
+
+F32 = mybir.dt.float32
+BF16 = mybir.dt.bfloat16
+I32 = mybir.dt.int32
+U32 = mybir.dt.uint32
+U16 = mybir.dt.uint16
+U8 = mybir.dt.uint8
+E4M3 = mybir.dt.float8_e4m3fn_x4
+E5M2 = mybir.dt.float8_e5m2_x4
+E2M1 = mybir.dt.float4_e2m1fn_x4
+ALU = mybir.AluOpType
+ACT = mybir.ActivationFunctionType
+AX = mybir.AxisListType
+
+P = 128
+H = 128
+
+
+def tile_list_outcomeneighbours_twotab_kernel(tc, xt_words, xt_scales, w_words, w_scales, xo_words, xo_scales, w2_words, w2_scales, wb_words, wb_scales, wc_words, wc_scales, so, offs, offs2, offs3, out):
+    nc = tc.nc
+    with ExitStack() as ctx:
+        sb = ctx.enter_context(tc.tile_pool(name="sb", bufs=1))
+        ps = ctx.enter_context(tc.psum_pool(name="ps", bufs=1))
+
+        def tile(name, shape, dt):
+            return sb.tile(shape, dt, name=name, align_bytes=64)
+
+        l1 = tile("l1", [P, 16], U16)
+        l2 = tile("l2", [P, 16], U16)
+        l3 = tile("l3", [P, 16], U16)
+        xtw = tile("xtw", [P, T], U32)
+        xow = tile("xow", [P, T], U32)
+        xts = tile("xts", [P, T], U8)
+        xos = tile("xos", [P, T], U8)
+        ww = tile("ww", [P, 2 * R], U8)
+        w2w = tile("w2w", [P, 2 * R], U8)
+        wbw = tile("wbw", [P, 2 * N], U8)
+        wcw = tile("wcw", [P, N], U32)
+        sot = tile("sot", [P, 2], F32)
+
+        def first_product(bank, wd, wsd, gw, gs, fmt, h):
+            c = slice(h * H, (h + 1) * H)
+            for t in range(4):
+                nc.tensor.matmul_mx(out=bank[:, t, :], lhsT=wd[:, 256 * t : 256 * (t + 1)].bitcast(E2M1), lhsT_scale=wsd[:, 128 * t : 128 * (t + 1)], rhs=gw[:, c].bitcast(fmt), rhs_scale=gs[:, c], start=True, stop=True)
+
+        def deal_words(dst, src):
+            nc.scalar.copy(out=dst[:].bitcast(U16).rearrange("p (t m) -> p t m", t=4), in_=src[:].bitcast(U16).rearrange("p (m t) -> p t m", t=4))
+
+        def deal_scales(dst, src):
+            nc.gpsimd.tensor_copy(out=dst[:].rearrange("p (t m) -> p t m", t=4), in_=src.rearrange("p (m t) -> p t m", t=4))
+
+        def words(ap):
+            return ap[0].rearrange("p c r -> p (c r)").bitcast(I32)
+
+        wd = tile("wd", [P, 2 * R], U8)
+        w2d = tile("w2d", [P, 2 * R], U8)
+        wsd = tile("wsd", [P, R], U8)
+        w2sd = tile("w2sd", [P, R], U8)
+        gtw = tile("gtw", [P, J], U32)
+        gow = tile("gow", [P, J], U32)
+        gts = tile("gts", [P, J], U8)
+        gos = tile("gos", [P, J], U8)
+        pa = [ps.tile([P, 4, H], F32, name="pa%d" % h) for h in range(2)]
+        pb = [ps.tile([P, 4, H], F32, name="pb%d" % h) for h in range(2)]
+        bs = [tile("bs%d" % h, [P, H, 4], F32) for h in range(2)]
+
+        xosS = tile("xosS", [64, 2, T], U8)
+        xtsS = tile("xtsS", [64, 2, T], U8)
+        wsT = tile("wsT", [P, 2, R], U8)
+        w2sT = tile("w2sT", [P, 2, R], U8)
+        bcT = tile("bcT", [P, 2, N], U8)
+        wbs = bcT[:, 0, :]
+        wcs = bcT[:, 1, :]
+
+        def load_half(eng, dst, src, q):
+            eng.dma_start(out=dst.bitcast(I32), in_=src[0].rearrange("(u q r) c -> q r u c", u=2, q=2)[q].bitcast(I32))
+
+        def load_staged(eng, st, src):
+            for q in range(2):
+                load_half(eng, st[32 * q : 32 * q + 4, :, :], src, q)
+
+
+        nc.vector.memset(xosS[:].bitcast(I32), 0)
+        nc.gpsimd.memset(w2sT[:].bitcast(I32), 0)
+        nc.vector.memset(xtsS[:].bitcast(I32), 0)
+        nc.gpsimd.memset(wsT[:].bitcast(I32), 0)
+        nc.gpsimd.memset(bcT[:].bitcast(I32), 0)
+        nc.sync.dma_start(out=w2w[:].bitcast(I32), in_=w2_words[0].bitcast(I32))
+        nc.sync.dma_start(out=l2[:], in_=offs2)
+        load_staged(nc.sync, w2sT, w2_scales)
+        load_staged(nc.sync, xosS, xo_scales)
+        nc.sync.dma_start(out=xow[:].bitcast(I32), in_=words(xo_words))
+        nc.sync.dma_start(out=ww[:].bitcast(I32), in_=w_words[0].bitcast(I32))
+        nc.sync.dma_start(out=l1[:], in_=offs)
+        load_staged(nc.sync, wsT, w_scales)
+        load_staged(nc.sync, xtsS, xt_scales)
+        nc.sync.dma_start(out=xtw[:].bitcast(I32), in_=words(xt_words))
+        nc.sync.dma_start(out=wbw[:].bitcast(I32), in_=wb_words[0].bitcast(I32))
+        nc.sync.dma_start(out=wcw[:].bitcast(I32), in_=words(wc_words))
+        for q in range(4):
+            nc.sync.dma_start(out=bcT[32 * q : 32 * q + 4, 0, :].bitcast(I32), in_=wb_scales[0, 4 * q : 4 * q + 4, :].bitcast(I32))
+            nc.sync.dma_start(out=bcT[32 * q : 32 * q + 4, 1, :].bitcast(I32), in_=wc_scales[0, 4 * q : 4 * q + 4, :].bitcast(I32))
+        nc.sync.dma_start(out=l3[:], in_=offs3)
+        with nc.allow_non_contiguous_dma(reason="one weight a partition"):
+            nc.sync.dma_start(out=sot[:], in_=so.rearrange("(s p) o -> p (s o)", p=P))
+
+        def mv(dst, src):
+            nc.vector.tensor_copy(out=dst.bitcast(I32), in_=src.bitcast(I32))
+
+        mv(w2sT[64:128, 0, :], w2sT[0:64, 1, :])
+        mv(xos[64:128, :], xosS[:, 1, :])
+        mv(xos[0:64, :], xosS[:, 0, :])
+        deal_words(w2d, w2w)
+        deal_scales(w2sd, w2sT[:, 0, :])
+        nc.vector.tensor_copy(out=gos[:], in_=xos[:].indirect(l2[:]))
+        nc.vector.tensor_copy(out=gow[:], in_=xow[:].indirect(l2[:]))
+        deal_words(wd, ww)
+        for h in range(2):
+            first_product(pb[h], w2d, w2sd, gow, gos, E4M3, h)
+            nc.scalar.copy(out=bs[h][:], in_=pb[h][:].rearrange("p t j -> p j t"))
+        mv(wsT[64:128, 0, :], wsT[0:64, 1, :])
+        mv(xts[64:128, :], xtsS[:, 1, :])
+        mv(xts[0:64, :], xtsS[:, 0, :])
+        deal_scales(wsd, wsT[:, 0, :])
+        for h in range(2):
+            nc.vector.tensor_copy(out=gtw[:, h * H : (h + 1) * H], in_=xtw[:].indirect(l1[:, 8 * h : 8 * (h + 1)]))
+            nc.vector.tensor_copy(out=gts[:, h * H : (h + 1) * H], in_=xts[:].indirect(l1[:, 8 * h : 8 * (h + 1)]))
+            first_product(pa[h], wd, wsd, gtw, gts, E5M2, h)
+
+        hid = [tile("hid%d" % h, [P, H, 4], BF16) for h in range(2)]
+        hq = [tile("hq%d" % h, [P, H], U32) for h in range(2)]
+        hs = [tile("hs%d" % h, [P, H], U8) for h in range(2)]
+        dd = [tile("dd%d" % h, [P, H, 4], F32) for h in range(2)]
+        m0 = [tile("m0_%d" % n, [P, J], F32) for n in range(2)]
+        pq = [[ps.tile([P, 2, H], F32, name="pq%d%d" % (n, h)) for h in range(2)] for n in range(2)]
+
+        def sub(h, c):
+            nc.vector.tensor_tensor(out=dd[h][:, c, :], in0=pa[h][:, :, c].rearrange("p t j -> p j t"), in1=bs[h][:, c, :], op=ALU.subtract)
+
+        def abs_s(h, c):
+            nc.scalar.activation(out=hid[h][:, c, :], in_=dd[h][:, c, :], func=ACT.Abs)
+
+        def abs_v(h, c):
+            nc.vector.scalar_tensor_tensor(out=hid[h][:, c, :], in0=dd[h][:, c, :], scalar=-1.0, in1=dd[h][:, c, :], op0=ALU.mult, op1=ALU.max)
+
+        def second(h):
+            nc.vector.quantize_mx(out=hq[h][:].bitcast(E4M3), scales=hs[h][:], in_=hid[h][:].rearrange("p j t -> p (j t)"))
+            for n in range(2):
+                nc.tensor.matmul_mx(out=pq[n][h][:, 0, :], lhsT=wbw[:, 256 * n : 256 * (n + 1)].bitcast(E2M1), lhsT_scale=wbs[:, 128 * n : 128 * (n + 1)], rhs=hq[h][:].bitcast(E4M3), rhs_scale=hs[h][:], start=True, stop=True)
+                nc.tensor.matmul_mx(out=pq[n][h][:, 1, :], lhsT=wcw[:, 128 * n : 128 * (n + 1)].bitcast(E4M3), lhsT_scale=wcs[:, 128 * n : 128 * (n + 1)], rhs=hq[h][:].bitcast(E4M3), rhs_scale=hs[h][:], start=True, stop=True)
+
+        lo, hi = slice(0, 64), slice(64, 128)
+        SP = 64
+        sub(0, lo)
+        abs_s(0, lo)
+        sub(0, hi)
+        abs_s(0, hi)
+        sub(1, slice(0, SP))
+        abs_s(1, slice(0, SP))
+        sub(1, slice(SP, H))
+        second(0)
+        abs_v(1, slice(SP, H))
+        second(1)
+        for n in range(2):
+            for h in range(2):
+                nc.vector.tensor_reduce(out=m0[n][:, h * H : (h + 1) * H], in_=pq[n][h][:].rearrange("p s j -> p j s"), axis=AX.X, op=ALU.max)
+        gg = [tile("gg%d" % n, [P, J], F32) for n in range(2)]
+        yy = [tile("yy%d" % n, [P, J], F32) for n in range(2)]
+        for n in range(2):
+            for h in range(2):
+                c = slice(h * H, (h + 1) * H)
+                nc.scalar.activation(out=gg[n][:, c], in_=m0[n][:].indirect(l3[:, 8 * h : 8 * (h + 1)]), func=ACT.Copy, scale=sot[:, n : n + 1])
+                nc.vector.tensor_tensor(out=yy[n][:, c], in0=m0[n][:, c], in1=gg[n][:, c], op=ALU.subtract)
+                if n == 1:
+                    nc.sync.dma_start(out=out[P * n : P * (n + 1), c], in_=yy[n][:, c])
+            if n == 0:
+                nc.sync.dma_start(out=out[P * n : P * (n + 1), :], in_=yy[n][:])

@@ -71,7 +71,6 @@ def tile_list_outcomeneighbours_twotab_kernel(tc, xt_words, xt_scales, w_words, 
         bs = [tile("bs%d" % h, [P, H, 4], F32) for h in range(2)]
 
         xosS = tile("xosS", [64, 2, T], U8)
-        xtsS = tile("xtsS", [64, 2, T], U8)
         wsT = tile("wsT", [P, 2, R], U8)
         w2sT = tile("w2sT", [P, 2, R], U8)
         bcT = tile("bcT", [P, 2, N], U8)
@@ -88,9 +87,9 @@ def tile_list_outcomeneighbours_twotab_kernel(tc, xt_words, xt_scales, w_words, 
 
         nc.vector.memset(xosS[:].bitcast(I32), 0)
         nc.gpsimd.memset(w2sT[:].bitcast(I32), 0)
-        nc.vector.memset(xtsS[:].bitcast(I32), 0)
-        nc.gpsimd.memset(wsT[:].bitcast(I32), 0)
-        nc.gpsimd.memset(bcT[:].bitcast(I32), 0)
+        nc.vector.memset(wsT[:].bitcast(I32), 0)
+        nc.vector.memset(xts[:].bitcast(I32), 0)
+        nc.vector.memset(bcT[:].bitcast(I32), 0)
         nc.sync.dma_start(out=w2w[:].bitcast(I32), in_=w2_words[0].bitcast(I32))
         nc.sync.dma_start(out=l2[:], in_=offs2)
         load_staged(nc.sync, w2sT, w2_scales)
@@ -99,8 +98,9 @@ def tile_list_outcomeneighbours_twotab_kernel(tc, xt_words, xt_scales, w_words, 
         nc.sync.dma_start(out=ww[:].bitcast(I32), in_=w_words[0].bitcast(I32))
         nc.sync.dma_start(out=l1[:], in_=offs)
         load_staged(nc.sync, wsT, w_scales)
-        load_staged(nc.sync, xtsS, xt_scales)
         nc.sync.dma_start(out=xtw[:].bitcast(I32), in_=words(xt_words))
+        for r in range(4):
+            nc.sync.dma_start(out=xts[r:P:32, :].bitcast(I32), in_=xt_scales[0].rearrange("(q r) c -> r q c", r=4)[r].bitcast(I32))
         nc.sync.dma_start(out=wbw[:].bitcast(I32), in_=wb_words[0].bitcast(I32))
         nc.sync.dma_start(out=wcw[:].bitcast(I32), in_=words(wc_words))
         for q in range(4):
@@ -125,11 +125,9 @@ def tile_list_outcomeneighbours_twotab_kernel(tc, xt_words, xt_scales, w_words, 
             first_product(pb[h], w2d, w2sd, gow, gos, E4M3, h)
             nc.scalar.copy(out=bs[h][:], in_=pb[h][:].rearrange("p t j -> p j t"))
         mv(wsT[64:128, 0, :], wsT[0:64, 1, :])
-        mv(xts[64:128, :], xtsS[:, 1, :])
-        mv(xts[0:64, :], xtsS[:, 0, :])
         deal_scales(wsd, wsT[:, 0, :])
+        nc.vector.tensor_copy(out=gtw[:], in_=xtw[:].indirect(l1[:]))
         for h in range(2):
-            nc.vector.tensor_copy(out=gtw[:, h * H : (h + 1) * H], in_=xtw[:].indirect(l1[:, 8 * h : 8 * (h + 1)]))
             nc.vector.tensor_copy(out=gts[:, h * H : (h + 1) * H], in_=xts[:].indirect(l1[:, 8 * h : 8 * (h + 1)]))
             first_product(pa[h], wd, wsd, gtw, gts, E5M2, h)
 
@@ -149,11 +147,12 @@ def tile_list_outcomeneighbours_twotab_kernel(tc, xt_words, xt_scales, w_words, 
         def abs_v(h, c):
             nc.vector.scalar_tensor_tensor(out=hid[h][:, c, :], in0=dd[h][:, c, :], scalar=-1.0, in1=dd[h][:, c, :], op0=ALU.mult, op1=ALU.max)
 
-        def second(h):
+        def quantise(h):
             nc.vector.quantize_mx(out=hq[h][:].bitcast(E4M3), scales=hs[h][:], in_=hid[h][:].rearrange("p j t -> p (j t)"))
-            for n in range(2):
-                nc.tensor.matmul_mx(out=pq[n][h][:, 0, :], lhsT=wbw[:, 256 * n : 256 * (n + 1)].bitcast(E2M1), lhsT_scale=wbs[:, 128 * n : 128 * (n + 1)], rhs=hq[h][:].bitcast(E4M3), rhs_scale=hs[h][:], start=True, stop=True)
-                nc.tensor.matmul_mx(out=pq[n][h][:, 1, :], lhsT=wcw[:, 128 * n : 128 * (n + 1)].bitcast(E4M3), lhsT_scale=wcs[:, 128 * n : 128 * (n + 1)], rhs=hq[h][:].bitcast(E4M3), rhs_scale=hs[h][:], start=True, stop=True)
+
+        def second(n, h):
+            nc.tensor.matmul_mx(out=pq[n][h][:, 0, :], lhsT=wbw[:, 256 * n : 256 * (n + 1)].bitcast(E2M1), lhsT_scale=wbs[:, 128 * n : 128 * (n + 1)], rhs=hq[h][:].bitcast(E4M3), rhs_scale=hs[h][:], start=True, stop=True)
+            nc.tensor.matmul_mx(out=pq[n][h][:, 1, :], lhsT=wcw[:, 128 * n : 128 * (n + 1)].bitcast(E4M3), lhsT_scale=wcs[:, 128 * n : 128 * (n + 1)], rhs=hq[h][:].bitcast(E4M3), rhs_scale=hs[h][:], start=True, stop=True)
 
         lo, hi = slice(0, 64), slice(64, 128)
         SP = 64
@@ -164,9 +163,12 @@ def tile_list_outcomeneighbours_twotab_kernel(tc, xt_words, xt_scales, w_words, 
         sub(1, slice(0, SP))
         abs_s(1, slice(0, SP))
         sub(1, slice(SP, H))
-        second(0)
+        quantise(0)
         abs_v(1, slice(SP, H))
-        second(1)
+        quantise(1)
+        for n in range(2):
+            for h in range(2):
+                second(n, h)
         for n in range(2):
             for h in range(2):
                 nc.vector.tensor_reduce(out=m0[n][:, h * H : (h + 1) * H], in_=pq[n][h][:].rearrange("p s j -> p j s"), axis=AX.X, op=ALU.max)

from contextlib import ExitStack

import concourse.mybir as mybir

K, T, J, R, N = 512, 1024, 256, 512, 256
FLOPS = 2 * K * R * J * 2 + 2 * R * N * J * 2

F32 = mybir.dt.float32
BF16 = mybir.dt.bfloat16
I32 = mybir.dt.int32
U32 = mybir.dt.uint32
U16 = mybir.dt.uint16
U8 = mybir.dt.uint8
E4M3 = mybir.dt.float8_e4m3fn_x4
E5M2 = mybir.dt.float8_e5m2_x4
E2M1 = mybir.dt.float4_e2m1fn_x4
ALU = mybir.AluOpType
ACT = mybir.ActivationFunctionType
AX = mybir.AxisListType

P = 128
H = 128


def tile_list_outcomeneighbours_twotab_kernel(tc, xt_words, xt_scales, w_words, w_scales, xo_words, xo_scales, w2_words, w2_scales, wb_words, wb_scales, wc_words, wc_scales, so, offs, offs2, offs3, out):
    nc = tc.nc
    with ExitStack() as ctx:
        sb = ctx.enter_context(tc.tile_pool(name="sb", bufs=1))
        ps = ctx.enter_context(tc.psum_pool(name="ps", bufs=1))

        def tile(name, shape, dt):
            return sb.tile(shape, dt, name=name, align_bytes=64)

        l1 = tile("l1", [P, 16], U16)
        l2 = tile("l2", [P, 16], U16)
        l3 = tile("l3", [P, 16], U16)
        xtw = tile("xtw", [P, T], U32)
        xow = tile("xow", [P, T], U32)
        xts = tile("xts", [P, T], U8)
        xos = tile("xos", [P, T], U8)
        ww = tile("ww", [P, 2 * R], U8)
        w2w = tile("w2w", [P, 2 * R], U8)
        wbw = tile("wbw", [P, 2 * N], U8)
        wcw = tile("wcw", [P, N], U32)
        sot = tile("sot", [P, 2], F32)

        def first_product(bank, wd, wsd, gw, gs, fmt, h):
            c = slice(h * H, (h + 1) * H)
            for t in range(4):
                nc.tensor.matmul_mx(out=bank[:, t, :], lhsT=wd[:, 256 * t : 256 * (t + 1)].bitcast(E2M1), lhsT_scale=wsd[:, 128 * t : 128 * (t + 1)], rhs=gw[:, c].bitcast(fmt), rhs_scale=gs[:, c], start=True, stop=True)

        def deal_words(dst, src):
            nc.scalar.copy(out=dst[:].bitcast(U16).rearrange("p (t m) -> p t m", t=4), in_=src[:].bitcast(U16).rearrange("p (m t) -> p t m", t=4))

        def deal_scales(dst, src):
            nc.gpsimd.tensor_copy(out=dst[:].rearrange("p (t m) -> p t m", t=4), in_=src.rearrange("p (m t) -> p t m", t=4))

        def words(ap):
            return ap[0].rearrange("p c r -> p (c r)").bitcast(I32)

        wd = tile("wd", [P, 2 * R], U8)
        w2d = tile("w2d", [P, 2 * R], U8)
        wsd = tile("wsd", [P, R], U8)
        w2sd = tile("w2sd", [P, R], U8)
        gtw = tile("gtw", [P, J], U32)
        gow = tile("gow", [P, J], U32)
        gts = tile("gts", [P, J], U8)
        gos = tile("gos", [P, J], U8)
        pa = [ps.tile([P, 4, H], F32, name="pa%d" % h) for h in range(2)]
        pb = [ps.tile([P, 4, H], F32, name="pb%d" % h) for h in range(2)]
        bs = [tile("bs%d" % h, [P, H, 4], F32) for h in range(2)]

        xosS = tile("xosS", [64, 2, T], U8)
        wsT = tile("wsT", [P, 2, R], U8)
        w2sT = tile("w2sT", [P, 2, R], U8)
        bcT = tile("bcT", [P, 2, N], U8)
        wbs = bcT[:, 0, :]
        wcs = bcT[:, 1, :]

        def load_half(eng, dst, src, q):
            eng.dma_start(out=dst.bitcast(I32), in_=src[0].rearrange("(u q r) c -> q r u c", u=2, q=2)[q].bitcast(I32))

        def load_staged(eng, st, src):
            for q in range(2):
                load_half(eng, st[32 * q : 32 * q + 4, :, :], src, q)


        nc.vector.memset(xosS[:].bitcast(I32), 0)
        nc.gpsimd.memset(w2sT[:].bitcast(I32), 0)
        nc.vector.memset(wsT[:].bitcast(I32), 0)
        nc.vector.memset(xts[:].bitcast(I32), 0)
        nc.vector.memset(bcT[:].bitcast(I32), 0)
        nc.sync.dma_start(out=w2w[:].bitcast(I32), in_=w2_words[0].bitcast(I32))
        nc.sync.dma_start(out=l2[:], in_=offs2)
        load_staged(nc.sync, w2sT, w2_scales)
        load_staged(nc.sync, xosS, xo_scales)
        nc.sync.dma_start(out=xow[:].bitcast(I32), in_=words(xo_words))
        nc.sync.dma_start(out=ww[:].bitcast(I32), in_=w_words[0].bitcast(I32))
        nc.sync.dma_start(out=l1[:], in_=offs)
        load_staged(nc.sync, wsT, w_scales)
        nc.sync.dma_start(out=xtw[:].bitcast(I32), in_=words(xt_words))
        for r in range(4):
            nc.sync.dma_start(out=xts[r:P:32, :].bitcast(I32), in_=xt_scales[0].rearrange("(q r) c -> r q c", r=4)[r].bitcast(I32))
        nc.sync.dma_start(out=wbw[:].bitcast(I32), in_=wb_words[0].bitcast(I32))
        nc.sync.dma_start(out=wcw[:].bitcast(I32), in_=words(wc_words))
        for q in range(4):
            nc.sync.dma_start(out=bcT[32 * q : 32 * q + 4, 0, :].bitcast(I32), in_=wb_scales[0, 4 * q : 4 * q + 4, :].bitcast(I32))
            nc.sync.dma_start(out=bcT[32 * q : 32 * q + 4, 1, :].bitcast(I32), in_=wc_scales[0, 4 * q : 4 * q + 4, :].bitcast(I32))
        nc.sync.dma_start(out=l3[:], in_=offs3)
        with nc.allow_non_contiguous_dma(reason="one weight a partition"):
            nc.sync.dma_start(out=sot[:], in_=so.rearrange("(s p) o -> p (s o)", p=P))

        def mv(dst, src):
            nc.vector.tensor_copy(out=dst.bitcast(I32), in_=src.bitcast(I32))

        mv(w2sT[64:128, 0, :], w2sT[0:64, 1, :])
        mv(xos[64:128, :], xosS[:, 1, :])
        mv(xos[0:64, :], xosS[:, 0, :])
        deal_words(w2d, w2w)
        deal_scales(w2sd, w2sT[:, 0, :])
        nc.vector.tensor_copy(out=gos[:], in_=xos[:].indirect(l2[:]))
        nc.vector.tensor_copy(out=gow[:], in_=xow[:].indirect(l2[:]))
        deal_words(wd, ww)
        for h in range(2):
            first_product(pb[h], w2d, w2sd, gow, gos, E4M3, h)
            nc.scalar.copy(out=bs[h][:], in_=pb[h][:].rearrange("p t j -> p j t"))
        mv(wsT[64:128, 0, :], wsT[0:64, 1, :])
        deal_scales(wsd, wsT[:, 0, :])
        nc.vector.tensor_copy(out=gtw[:], in_=xtw[:].indirect(l1[:]))
        for h in range(2):
            nc.vector.tensor_copy(out=gts[:, h * H : (h + 1) * H], in_=xts[:].indirect(l1[:, 8 * h : 8 * (h + 1)]))
            first_product(pa[h], wd, wsd, gtw, gts, E5M2, h)

        hid = [tile("hid%d" % h, [P, H, 4], BF16) for h in range(2)]
        hq = [tile("hq%d" % h, [P, H], U32) for h in range(2)]
        hs = [tile("hs%d" % h, [P, H], U8) for h in range(2)]
        dd = [tile("dd%d" % h, [P, H, 4], F32) for h in range(2)]
        m0 = [tile("m0_%d" % n, [P, J], F32) for n in range(2)]
        pq = [[ps.tile([P, 2, H], F32, name="pq%d%d" % (n, h)) for h in range(2)] for n in range(2)]

        def sub(h, c):
            nc.vector.tensor_tensor(out=dd[h][:, c, :], in0=pa[h][:, :, c].rearrange("p t j -> p j t"), in1=bs[h][:, c, :], op=ALU.subtract)

        def abs_s(h, c):
            nc.scalar.activation(out=hid[h][:, c, :], in_=dd[h][:, c, :], func=ACT.Abs)

        def abs_v(h, c):
            nc.vector.scalar_tensor_tensor(out=hid[h][:, c, :], in0=dd[h][:, c, :], scalar=-1.0, in1=dd[h][:, c, :], op0=ALU.mult, op1=ALU.max)

        def quantise(h):
            nc.vector.quantize_mx(out=hq[h][:].bitcast(E4M3), scales=hs[h][:], in_=hid[h][:].rearrange("p j t -> p (j t)"))

        def second(n, h):
            nc.tensor.matmul_mx(out=pq[n][h][:, 0, :], lhsT=wbw[:, 256 * n : 256 * (n + 1)].bitcast(E2M1), lhsT_scale=wbs[:, 128 * n : 128 * (n + 1)], rhs=hq[h][:].bitcast(E4M3), rhs_scale=hs[h][:], start=True, stop=True)
            nc.tensor.matmul_mx(out=pq[n][h][:, 1, :], lhsT=wcw[:, 128 * n : 128 * (n + 1)].bitcast(E4M3), lhsT_scale=wcs[:, 128 * n : 128 * (n + 1)], rhs=hq[h][:].bitcast(E4M3), rhs_scale=hs[h][:], start=True, stop=True)

        lo, hi = slice(0, 64), slice(64, 128)
        SP = 64
        sub(0, lo)
        abs_s(0, lo)
        sub(0, hi)
        abs_s(0, hi)
        sub(1, slice(0, SP))
        abs_s(1, slice(0, SP))
        sub(1, slice(SP, H))
        quantise(0)
        abs_v(1, slice(SP, H))
        quantise(1)
        for n in range(2):
            for h in range(2):
                second(n, h)
        for n in range(2):
            for h in range(2):
                nc.vector.tensor_reduce(out=m0[n][:, h * H : (h + 1) * H], in_=pq[n][h][:].rearrange("p s j -> p j s"), axis=AX.X, op=ALU.max)
        gg = [tile("gg%d" % n, [P, J], F32) for n in range(2)]
        yy = [tile("yy%d" % n, [P, J], F32) for n in range(2)]
        for n in range(2):
            for h in range(2):
                c = slice(h * H, (h + 1) * H)
                nc.scalar.activation(out=gg[n][:, c], in_=m0[n][:].indirect(l3[:, 8 * h : 8 * (h + 1)]), func=ACT.Copy, scale=sot[:, n : n + 1])
                nc.vector.tensor_tensor(out=yy[n][:, c], in0=m0[n][:, c], in1=gg[n][:, c], op=ALU.subtract)
                if n == 1:
                    nc.sync.dma_start(out=out[P * n : P * (n + 1), c], in_=yy[n][:, c])
            if n == 0:
                nc.sync.dma_start(out=out[P * n : P * (n + 1), :], in_=yy[n][:])
